import numpy as np
import ml_dtypes


def mxq(x, axis, fmt="e4m3"):
    dtype, down = {"e4m3": (ml_dtypes.float8_e4m3fn, 7), "e5m2": (ml_dtypes.float8_e5m2, 14)}[fmt]
    v = np.moveaxis(np.asarray(x, np.float32).astype(ml_dtypes.bfloat16).astype(np.float64), axis, -1)
    blocks = v.reshape(v.shape[:-1] + (-1, 32))
    amax = np.abs(blocks).max(-1, keepdims=True)
    byte = np.maximum(np.where(amax > 0, np.frexp(amax)[1] - 1 + 127, 0) - down, 1)
    scale = np.exp2(byte - 127.0)
    codes = (blocks / scale).astype(np.float32).astype(dtype).astype(np.float64)
    return np.moveaxis((codes * scale).reshape(v.shape), -1, axis)


WIDE = False


def mx_kscale(k):
    if not WIDE:
        return np.ones(k)
    levels = np.array([10, -10, 5, -5, 0])
    if k % 512:
        return np.exp2(np.random.permutation(np.resize(levels, k // 32))).repeat(32)
    a = np.empty((k // 512, 16))
    for p in range(k // 512):
        a[p, :8] = np.random.permutation(np.resize(levels, 8))
        for g in range(8):
            far = levels[np.abs(levels - a[p, g]) >= 10]
            a[p, g + 8] = far[np.random.randint(len(far))]
    return np.exp2(a.ravel()).repeat(32)


def f64(x):
    return np.asarray(x).astype(np.float64)


def striped(idx):
    return np.tile(np.asarray(idx).reshape(-1, 16).T, (8, 1)).astype(np.uint16)


def unstriped(offs):
    return offs[:16].T.reshape(-1).astype(np.int64)


E2M1 = np.array([0.0, 0.5, 1.0, 1.5, 2.0, 3.0, 4.0, 6.0, -0.0, -0.5, -1.0, -1.5, -2.0, -3.0, -4.0, -6.0])


def pack_weight(w, fmt):
    k, n = w.shape
    w = f64(np.asarray(w, np.float32).astype(ml_dtypes.bfloat16)).reshape(k // 32, 32, n)
    amax = np.abs(w).max(1)
    if fmt == "e4m3":
        byte = np.frexp(amax)[1] - 1 + 127 - 7
    else:
        mant, ex = np.frexp(amax / 6.0)
        byte = np.where(mant > 0.5, ex, ex - 1) + 127
    byte = np.clip(np.where(amax > 0, byte, 1), 1, 254)
    scaled = (w * np.exp2(127.0 - byte)[:, None, :]).reshape(k, n).astype(np.float32)
    by_word = np.ascontiguousarray(scaled.reshape(k // 512, 128, 4, n).transpose(0, 1, 3, 2))
    if fmt == "e4m3":
        words = by_word.astype(ml_dtypes.float8_e4m3fn).view(np.uint8)
    else:
        c = by_word.astype(ml_dtypes.float4_e2m1fn).view(np.uint8) & 0xF
        words = (c[..., 0::2] | (c[..., 1::2] << 4)).reshape(k // 512, 128, 2 * n)
    return np.ascontiguousarray(words), np.ascontiguousarray(byte.astype(np.uint8).reshape(k // 512, 16, n))


def unpack_weight(words, scales, fmt):
    g, _, n = scales.shape
    words = np.ascontiguousarray(words).reshape(g, 128, n, -1)
    if fmt == "e4m3":
        vals = words.view(ml_dtypes.float8_e4m3fn).astype(np.float64)
    else:
        nib = np.empty((g, 128, n, 4), np.uint8)
        nib[..., 0::2] = words & 0xF
        nib[..., 1::2] = words >> 4
        vals = E2M1[nib]
    vals = vals * np.repeat(np.exp2(scales.astype(np.float64) - 127.0), 8, axis=1)[..., None]
    return vals.transpose(0, 1, 3, 2).reshape(g * 512, n)


def sigmoid(v):
    return 1.0 / (1.0 + np.exp(-v))


D, T, I, Q, E, Z, M = 512, 2048, 512, 256, 512, 1024, 1024


def setup_inputs():
    n = np.random.standard_normal
    idx = np.random.permutation(T)[:I]
    idx2 = np.random.permutation(Z)[:I]
    idx3 = np.random.permutation(Z)[:I]
    idx4 = np.random.permutation(M)[:Q]
    fd = mx_kscale(D)
    fi = mx_kscale(I)
    ti = np.ones(T)
    ti[idx] = fi
    keysp = pack_weight(n((D, T)) / fd[:, None], "e2m1")
    return {
        "query": (n((D, Q)) * 1.0 / np.sqrt(D) * fd[:, None]).astype(np.float32),
        "keys_words": keysp[0],
        "keys_scales": keysp[1],
        "os": (np.random.uniform(0.02, 0.08, (1, I)) * fi).astype(np.float32),
        "vals": (n((E, T)) / ti).astype(np.float32),
        "old": (n((E, M)) * 2.0).astype(np.float32),
        "fade": (np.random.uniform(0.3, 0.9, (1, M))).astype(np.float32),
        "offs": striped(idx),
        "offs2": striped(idx2),
        "offs3": striped(idx3),
        "offs4": striped(idx4),
    }


def reference(query, keys_words, keys_scales, os, vals, old, fade, offs, offs2, offs3, offs4):
    idx = unstriped(offs)
    idx2 = unstriped(offs2)
    idx3 = unstriped(offs3)
    idx4 = unstriped(offs4)
    keysu = unpack_weight(keys_words, keys_scales, "e2m1")
    queryq = mxq(f64(query), 0, "e4m3")
    keysidxg = keysu[:, idx]
    a = queryq.T @ keysidxg
    f0 = np.zeros((Q, Z))
    f0[:, idx2] = a
    s = a + f0[:, idx3]
    w = sigmoid(s)
    wo1 = w * f64(os)
    wt1 = wo1.T
    vt1 = f64(vals)[:, idx].T
    vt1q = mxq(vt1, 0, "e4m3")
    wt1q = mxq(wt1, 0, "e4m3")
    o = vt1q.T @ wt1q
    of = np.zeros((E, M))
    of[:, idx4] = o
    y = f64(old) * f64(fade) + of
    return y

@@ -1,0 +1,258 @@
+from contextlib import ExitStack
+
+import concourse.mybir as mybir
+from concourse.masks import make_identity
+
+D, T, I, Q, E, Z, M = 512, 2048, 512, 256, 512, 1024, 1024
+FLOPS = 2 * D * Q * I + 2 * I * E * Q
+
+F32 = mybir.dt.float32
+BF16 = mybir.dt.bfloat16
+I32 = mybir.dt.int32
+U32 = mybir.dt.uint32
+U16 = mybir.dt.uint16
+U8 = mybir.dt.uint8
+FP8X4 = mybir.dt.float8_e4m3fn_x4
+FP4X4 = mybir.dt.float4_e2m1fn_x4
+MULT = mybir.AluOpType.mult
+ADD = mybir.AluOpType.add
+COPY = mybir.ActivationFunctionType.Copy
+SIGMOID = mybir.ActivationFunctionType.Sigmoid
+
+P = 128
+PACK = 4
+BANK = 512
+HALF = I // 2
+LIST_ROWS = 16
+
+
+def tile_attend_passedthrough_written_lean_kernel(
+    tc, query, keys_words, keys_scales, slot_factor, vals, old, fade, offs, offs2, offs3, offs4, out
+):
+    nc = tc.nc
+    q_tiles = Q // P
+    e_tiles = E // P
+    with ExitStack() as ctx:
+        sb = ctx.enter_context(tc.tile_pool(name="sb", bufs=1))
+        ps = ctx.enter_context(tc.psum_pool(name="ps", bufs=1))
+
+        def bank(tag):
+            return ps.tile([P, BANK], F32, name=tag, tag=tag)
+
+        idx = sb.tile([P, I // LIST_ROWS], U16, name="idx")
+        idx2 = sb.tile([P, I // LIST_ROWS], U16, name="idx2")
+        idx3 = sb.tile([P, I // LIST_ROWS], U16, name="idx3")
+        idx4 = sb.tile([P, Q // LIST_ROWS], U16, name="idx4")
+        key_words = sb.tile([P, T], U16, name="key_words", align_bytes=64)
+        key_scales = sb.tile([P, T], U8, name="key_scales", align_bytes=64)
+        query_raw = [sb.tile([P, PACK, P], F32, name="query_raw%d" % g, tag="query_raw%d" % g, align_bytes=64) for g in range(q_tiles)]
+        factor = sb.tile([P, PACK], F32, name="factor")
+        fade_cols = sb.tile([P, M // BANK, PACK], F32, name="fade_cols")
+        val_pool = [sb.tile([P, T], F32, name="val_pool%d" % c, tag="val_pool%d" % c, align_bytes=64) for c in range(e_tiles)]
+        kept = [sb.tile([P, M], F32, name="kept%d" % c) for c in range(e_tiles)]
+        places = [sb.tile([P, Z], F32, name="places%d" % g, tag="places%d" % g, align_bytes=64) for g in range(q_tiles)]
+        written = [sb.tile([P, M], F32, name="written%d" % c) for c in range(2)]
+        ident = sb.tile([P, P], F32, name="ident")
+
+        nc.gpsimd.memset(key_scales[:].bitcast(I32), 0)
+        nc.sync.dma_start(idx[:], offs)
+        nc.sync.dma_start(idx2[:], offs2)
+        nc.sync.dma_start(key_words[:].bitcast(I32), keys_words[0].bitcast(I32))
+        for quad in range(4):
+            nc.sync.dma_start(
+                key_scales[32 * quad : 32 * quad + 4, :].bitcast(I32),
+                keys_scales[0, 4 * quad : 4 * quad + 4, :].bitcast(I32),
+            )
+        for g in range(q_tiles):
+            nc.sync.dma_start(query_raw[g][:], query[:, g * P : (g + 1) * P].rearrange("(p j) q -> p j q", j=PACK))
+
+        def load_values(c):
+            nc.sync.dma_start(val_pool[c][:], vals[c * P : (c + 1) * P, :])
+
+        def load_old(c):
+            nc.sync.dma_start(kept[c][:], old[c * P : (c + 1) * P, :])
+
+        load_values(0)
+        nc.sync.dma_start(idx3[:], offs3)
+        nc.sync.dma_start(fade_cols[:], fade[0].rearrange("(h p j) -> p h j", p=P, j=PACK))
+        load_values(1)
+        nc.sync.dma_start(factor[:], slot_factor[0].rearrange("(p t) -> p t", t=PACK))
+        load_values(2)
+        load_old(0)
+        nc.sync.dma_start(idx4[:], offs4)
+        load_values(3)
+        for c in range(1, e_tiles):
+            load_old(c)
+
+        make_identity(nc, ident[:])
+        for g in range(q_tiles):
+            nc.vector.memset(places[g][:], 0.0)
+        for c in range(2):
+            nc.vector.memset(written[c][:], 0.0)
+
+        q_bf = [sb.tile([P, P, PACK], BF16, name="q_bf%d" % g, tag="q_bf%d" % g, align_bytes=64) for g in range(q_tiles)]
+        q_codes = [sb.tile([P, P], U32, name="q_codes%d" % g, tag="q_codes%d" % g, align_bytes=64) for g in range(q_tiles)]
+        q_scales = [sb.tile([P, P], U8, name="q_scales%d" % g, align_bytes=64) for g in range(q_tiles)]
+        got_words = []
+        got_scales = []
+
+        def half_list(lst, h):
+            return lst[:, h * HALF // LIST_ROWS : (h + 1) * HALF // LIST_ROWS]
+
+        def gather_keys(h):
+            words = sb.tile([P, HALF], U16, name="got_words%d" % h, tag="q_bf0" if h else "got_words", align_bytes=64)
+            scales = sb.tile([P, HALF], U8, name="got_scales%d" % h, tag="query_raw0" if h else "got_scales", align_bytes=64)
+            nc.vector.tensor_copy(words[:], key_words[:].indirect(half_list(idx, h)))
+            nc.vector.tensor_copy(scales[:], key_scales[:].indirect(half_list(idx, h)))
+            got_words.append(words)
+            got_scales.append(scales)
+
+        def quantize(codes, scales, rounded):
+            nc.vector.quantize_mx(out=codes.bitcast(FP8X4), scales=scales, in_=rounded)
+
+        for g in range(q_tiles):
+            nc.scalar.copy(q_bf[g][:], query_raw[g][:].rearrange("p j q -> p q j"))
+        gather_keys(0)
+        for g in range(q_tiles):
+            quantize(q_codes[g][:], q_scales[g][:], q_bf[g][:].rearrange("p q j -> p (q j)"))
+        gather_keys(1)
+
+        prod = sb.tile([P, q_tiles, I], F32, name="prod")
+
+        def score(dst, g, h):
+            nc.tensor.matmul_mx(
+                out=dst,
+                lhsT=q_codes[g][:].bitcast(FP8X4),
+                lhsT_scale=q_scales[g][:],
+                rhs=got_words[h][:].bitcast(FP4X4),
+                rhs_scale=got_scales[h][:],
+                start=True,
+                stop=True,
+            )
+
+        first, second = slice(0, HALF), slice(HALF, I)
+        acc = bank("early0")
+        score(acc[:, first], 0, 0)
+        nc.scalar.copy(prod[:, 0, first], acc[:, first])
+        nc.scalar.activation(places[0][:].indirect(half_list(idx2, 0)), prod[:, 0, first], COPY)
+        acc = bank("early1")
+        score(acc[:, first], 1, 0)
+        nc.vector.tensor_copy(prod[:, 1, first], acc[:, first])
+        nc.vector.tensor_copy(places[1][:].indirect(half_list(idx2, 0)), prod[:, 1, first])
+        acc = bank("early0")
+        for g in range(q_tiles):
+            score(acc[:, g * HALF : (g + 1) * HALF], g, 1)
+        nc.scalar.copy(prod[:, :, second], acc[:].rearrange("q (g i) -> q g i", g=q_tiles))
+        for g in range(q_tiles):
+            nc.scalar.activation(places[g][:].indirect(half_list(idx2, 1)), prod[:, g, second], COPY)
+
+        for tag in ("q_bf1", "q_codes1"):
+            late = sb.tile([P, M], F32, name="late_" + tag, tag=tag, align_bytes=64)
+            nc.gpsimd.memset(late[:], 0.0)
+            written.append(late)
+
+        fade_rows = []
+        for h in range(M // BANK):
+            rows = bank("fade%d" % h)
+            for j in range(PACK):
+                nc.tensor.transpose(
+                    rows[:, j * P : (j + 1) * P], fade_cols[:, h, j : j + 1].to_broadcast([P, P]), ident[:]
+                )
+            fade_rows.append(rows)
+
+        turned_values = {}
+        v_codes = {}
+        v_scales = {}
+
+        def gather_values(c):
+            picked = sb.tile([P, I], BF16, name="picked%d" % c, align_bytes=64)
+            if c == 0:
+                nc.vector.tensor_copy(picked[:], val_pool[c][:].indirect(idx[:]))
+            else:
+                nc.scalar.activation(picked[:], val_pool[c][:].indirect(idx[:]), COPY)
+            pairs = picked[:].bitcast(F32)
+            if c % 2 == 0:
+                turned_values[c // 2] = bank("turn%d" % (c // 2))
+            for u in range(2):
+                col = (2 * (c % 2) + u) * P
+                nc.tensor.transpose(turned_values[c // 2][:, col : col + P], pairs[:, u : I // 2 : 2], ident[:])
+
+        v_pairs = {}
+
+        def lay_values(pair):
+            v_pairs[pair] = sb.tile([P, 2, P, 2], F32, name="v_bf%d" % pair, align_bytes=64)
+            copy = nc.vector.tensor_copy if pair else nc.scalar.copy
+            copy(v_pairs[pair][:], turned_values[pair][:].rearrange("p (k u e) -> p k e u", k=2, u=2))
+
+        def quantize_values(pair):
+            v_bf = v_pairs[pair]
+            v_codes[pair] = sb.tile([P, 2 * P], U32, name="v_codes%d" % pair, tag="places%d" % (1 - pair), align_bytes=64)
+            v_scales[pair] = sb.tile([P, 2 * P], U8, name="v_scales%d" % pair, align_bytes=64)
+            quantize(v_codes[pair][:], v_scales[pair][:], v_bf[:].rearrange("p k e u -> p (k e u)").bitcast(BF16))
+
+        w_codes = sb.tile([P, Q], U32, name="w_codes", align_bytes=64)
+        w_scales = sb.tile([P, Q], U8, name="w_scales", align_bytes=64)
+
+        def weigh(g):
+            s = sb.tile([P, I], F32, name="s%d" % g, tag="s%d" % g, align_bytes=64)
+            nc.vector.tensor_tensor(s[:], places[g][:].indirect(idx3[:]), prod[:, g, :], ADD)
+            w = sb.tile([P, PACK, P], F32, name="w%d" % g, tag="val_pool1" if g else "w0", align_bytes=64)
+            nc.scalar.activation(w[:].rearrange("q t p -> q p t"), s[:].rearrange("q (p t) -> q p t", t=PACK), SIGMOID)
+            turned = bank("early%d" % g)
+            for t in range(PACK):
+                nc.tensor.transpose(turned[:, t * P : (t + 1) * P], w[:, t, :], ident[:])
+            w_bf = sb.tile([P, P, PACK], BF16, name="w_bf%d" % g, align_bytes=64)
+            nc.vector.tensor_tensor(
+                w_bf[:],
+                turned[:].rearrange("p (t q) -> p q t", t=PACK),
+                factor[:].unsqueeze(1).to_broadcast([P, P, PACK]),
+                MULT,
+            )
+            cols = slice(g * P, (g + 1) * P)
+            quantize(w_codes[:, cols], w_scales[:, cols], w_bf[:].rearrange("p q t -> p (q t)"))
+
+        gather_values(0)
+        weigh(0)
+        gather_values(1)
+        weigh(1)
+        lay_values(0)
+        quantize_values(0)
+        gather_values(2)
+        gather_values(3)
+        lay_values(1)
+        quantize_values(1)
+
+        def fade_old(c):
+            for h in range(M // BANK):
+                part = kept[c][:, h * BANK : (h + 1) * BANK].rearrange("e (n j) -> e n j", j=PACK)
+                nc.vector.tensor_tensor(part, part, fade_rows[h][:].rearrange("e (j n) -> e n j", j=PACK), MULT)
+
+        def products(pair):
+            acc = bank("turn%d" % pair)
+            for k in range(2):
+                nc.tensor.matmul_mx(
+                    out=acc[:, k * Q : (k + 1) * Q],
+                    lhsT=v_codes[pair][:, k * P : (k + 1) * P].bitcast(FP8X4),
+                    lhsT_scale=v_scales[pair][:, k * P : (k + 1) * P],
+                    rhs=w_codes[:].bitcast(FP8X4),
+                    rhs_scale=w_scales[:],
+                    start=True,
+                    stop=True,
+                )
+            o = sb.tile([P, 2 * Q], F32, name="o%d" % pair, tag="val_pool%d" % (3 - pair), align_bytes=64)
+            nc.scalar.copy(o[:], acc[:])
+            for k in range(2):
+                nc.scalar.activation(written[2 * pair + k][:].indirect(idx4[:]), o[:, k * Q : (k + 1) * Q], COPY)
+
+        def finish(c):
+            for h in range(M // BANK):
+                cols = slice(h * BANK, (h + 1) * BANK)
+                nc.vector.tensor_tensor(kept[c][:, cols], kept[c][:, cols], written[c][:, cols], ADD)
+                nc.sync.dma_start(out[c * P : (c + 1) * P, cols], kept[c][:, cols])
+
+        for pair in range(e_tiles // 2):
+            products(pair)
+        for c in range(e_tiles):
+            fade_old(c)
+        for c in range(e_tiles):
+            finish(c)

@@ -85,6 +85,8 @@ def tile_attend_passedthrough_written_lean_kernel(
             load_old(c)
 
         make_identity(nc, ident[:])
+        warm = sb.tile([P, 1], F32, name="warm")
+        nc.scalar.activation(warm[:], ident[:, 0:1], SIGMOID)
         for g in range(q_tiles):
             nc.vector.memset(places[g][:], 0.0)
         for c in range(2):

@@ -24,6 +24,7 @@ PACK = 4
 BANK = 512
 HALF = I // 2
 LIST_ROWS = 16
+WINDOWS = 2
 
 
 def tile_attend_passedthrough_written_lean_kernel(
@@ -47,14 +48,15 @@ def tile_attend_passedthrough_written_lean_kernel(
         key_scales = sb.tile([P, T], U8, name="key_scales", align_bytes=64)
         query_raw = [sb.tile([P, PACK, P], F32, name="query_raw%d" % g, tag="query_raw%d" % g, align_bytes=64) for g in range(q_tiles)]
         factor = sb.tile([P, PACK], F32, name="factor")
-        fade_cols = sb.tile([P, M // BANK, PACK], F32, name="fade_cols")
+        fade_blocks = sb.tile([P, P], F32, name="fade_blocks")
         val_pool = [sb.tile([P, T], F32, name="val_pool%d" % c, tag="val_pool%d" % c, align_bytes=64) for c in range(e_tiles)]
         kept = [sb.tile([P, M], F32, name="kept%d" % c) for c in range(e_tiles)]
         places = [sb.tile([P, Z], F32, name="places%d" % g, tag="places%d" % g, align_bytes=64) for g in range(q_tiles)]
-        written = [sb.tile([P, M], F32, name="written%d" % c) for c in range(2)]
+        written = [sb.tile([P, M], F32, name="written%d" % c) for c in range(WINDOWS)]
         ident = sb.tile([P, P], F32, name="ident")
 
         nc.gpsimd.memset(key_scales[:].bitcast(I32), 0)
+        nc.gpsimd.memset(fade_blocks[:], 0.0)
         nc.sync.dma_start(idx[:], offs)
         nc.sync.dma_start(idx2[:], offs2)
         nc.sync.dma_start(key_words[:].bitcast(I32), keys_words[0].bitcast(I32))
@@ -74,7 +76,7 @@ def tile_attend_passedthrough_written_lean_kernel(
 
         load_values(0)
         nc.sync.dma_start(idx3[:], offs3)
-        nc.sync.dma_start(fade_cols[:], fade[0].rearrange("(h p j) -> p h j", p=P, j=PACK))
+        nc.sync.dma_start(fade_blocks[0 : M // P, :], fade[0].rearrange("(b p) -> b p", p=P))
         load_values(1)
         nc.sync.dma_start(factor[:], slot_factor[0].rearrange("(p t) -> p t", t=PACK))
         load_values(2)
@@ -89,7 +91,7 @@ def tile_attend_passedthrough_written_lean_kernel(
         nc.scalar.activation(warm[:], ident[:, 0:1], SIGMOID)
         for g in range(q_tiles):
             nc.vector.memset(places[g][:], 0.0)
-        for c in range(2):
+        for c in range(WINDOWS):
             nc.vector.memset(written[c][:], 0.0)
 
         q_bf = [sb.tile([P, P, PACK], BF16, name="q_bf%d" % g, tag="q_bf%d" % g, align_bytes=64) for g in range(q_tiles)]
@@ -148,17 +150,16 @@ def tile_attend_passedthrough_written_lean_kernel(
         for g in range(q_tiles):
             nc.scalar.activation(places[g][:].indirect(half_list(idx2, 1)), prod[:, g, second], COPY)
 
-        for tag in ("q_bf1", "q_codes1"):
-            late = sb.tile([P, M], F32, name="late_" + tag, tag=tag, align_bytes=64)
-            nc.gpsimd.memset(late[:], 0.0)
-            written.append(late)
-
+        turned_fade = bank("fade1")
+        nc.tensor.transpose(turned_fade[:, 0:P], fade_blocks[:], ident[:])
+        fade_cols = sb.tile([P, M // P], F32, name="fade_cols")
+        nc.vector.tensor_copy(fade_cols[:], turned_fade[:, 0 : M // P])
         fade_rows = []
         for h in range(M // BANK):
             rows = bank("fade%d" % h)
             for j in range(PACK):
                 nc.tensor.transpose(
-                    rows[:, j * P : (j + 1) * P], fade_cols[:, h, j : j + 1].to_broadcast([P, P]), ident[:]
+                    rows[:, j * P : (j + 1) * P], fade_cols[:, PACK * h + j : PACK * h + j + 1].to_broadcast([P, P]), ident[:]
                 )
             fade_rows.append(rows)
 
@@ -226,8 +227,10 @@ def tile_attend_passedthrough_written_lean_kernel(
 
         def fade_old(c):
             for h in range(M // BANK):
-                part = kept[c][:, h * BANK : (h + 1) * BANK].rearrange("e (n j) -> e n j", j=PACK)
-                nc.vector.tensor_tensor(part, part, fade_rows[h][:].rearrange("e (j n) -> e n j", j=PACK), MULT)
+                part = kept[c][:, h * BANK : (h + 1) * BANK]
+                nc.vector.tensor_tensor(part, part, fade_rows[h][:], MULT)
+
+        results = []
 
         def products(pair):
             acc = bank("turn%d" % pair)
@@ -243,18 +246,27 @@ def tile_attend_passedthrough_written_lean_kernel(
                 )
             o = sb.tile([P, 2 * Q], F32, name="o%d" % pair, tag="val_pool%d" % (3 - pair), align_bytes=64)
             nc.scalar.copy(o[:], acc[:])
-            for k in range(2):
-                nc.scalar.activation(written[2 * pair + k][:].indirect(idx4[:]), o[:, k * Q : (k + 1) * Q], COPY)
+            results.extend(o[:, k * Q : (k + 1) * Q] for k in range(2))
 
-        def finish(c):
-            for h in range(M // BANK):
-                cols = slice(h * BANK, (h + 1) * BANK)
-                nc.vector.tensor_tensor(kept[c][:, cols], kept[c][:, cols], written[c][:, cols], ADD)
+        def write(c):
+            nc.scalar.activation(written[c % WINDOWS][:].indirect(idx4[:]), results[c], COPY)
+
+        def finish(c, width):
+            for col in range(0, M, width):
+                cols = slice(col, col + width)
+                nc.vector.tensor_tensor(kept[c][:, cols], kept[c][:, cols], written[c % WINDOWS][:, cols], ADD)
                 nc.sync.dma_start(out[c * P : (c + 1) * P, cols], kept[c][:, cols])
 
-        for pair in range(e_tiles // 2):
-            products(pair)
-        for c in range(e_tiles):
+        products(0)
+        write(0)
+        write(1)
+        products(1)
+        for c in range(3):
             fade_old(c)
-        for c in range(e_tiles):
-            finish(c)
+        finish(0, M)
+        write(2)
+        finish(1, M)
+        write(3)
+        fade_old(3)
+        finish(2, BANK)
+        finish(3, BANK // 2)

@@ -48,15 +48,14 @@ def tile_attend_passedthrough_written_lean_kernel(
         key_scales = sb.tile([P, T], U8, name="key_scales", align_bytes=64)
         query_raw = [sb.tile([P, PACK, P], F32, name="query_raw%d" % g, tag="query_raw%d" % g, align_bytes=64) for g in range(q_tiles)]
         factor = sb.tile([P, PACK], F32, name="factor")
-        fade_blocks = sb.tile([P, P], F32, name="fade_blocks")
+        fade_cols = sb.tile([P, M // BANK, PACK], F32, name="fade_cols")
         val_pool = [sb.tile([P, T], F32, name="val_pool%d" % c, tag="val_pool%d" % c, align_bytes=64) for c in range(e_tiles)]
         kept = [sb.tile([P, M], F32, name="kept%d" % c) for c in range(e_tiles)]
         places = [sb.tile([P, Z], F32, name="places%d" % g, tag="places%d" % g, align_bytes=64) for g in range(q_tiles)]
-        written = [sb.tile([P, M], F32, name="written%d" % c) for c in range(WINDOWS)]
+        written = [sb.tile([P, M], F32, name="written%d" % c, tag="written%d" % c) for c in range(WINDOWS)]
         ident = sb.tile([P, P], F32, name="ident")
 
         nc.gpsimd.memset(key_scales[:].bitcast(I32), 0)
-        nc.gpsimd.memset(fade_blocks[:], 0.0)
         nc.sync.dma_start(idx[:], offs)
         nc.sync.dma_start(idx2[:], offs2)
         nc.sync.dma_start(key_words[:].bitcast(I32), keys_words[0].bitcast(I32))
@@ -75,15 +74,16 @@ def tile_attend_passedthrough_written_lean_kernel(
             nc.sync.dma_start(kept[c][:], old[c * P : (c + 1) * P, :])
 
         load_values(0)
-        nc.sync.dma_start(idx3[:], offs3)
-        nc.sync.dma_start(fade_blocks[0 : M // P, :], fade[0].rearrange("(b p) -> b p", p=P))
+        nc.sync.dma_start(fade_cols[:], fade[0].rearrange("(h p j) -> p h j", p=P, j=PACK))
         load_values(1)
         nc.sync.dma_start(factor[:], slot_factor[0].rearrange("(p t) -> p t", t=PACK))
-        load_values(2)
         load_old(0)
+        nc.sync.dma_start(idx3[:], offs3)
+        load_old(1)
+        load_values(2)
         nc.sync.dma_start(idx4[:], offs4)
         load_values(3)
-        for c in range(1, e_tiles):
+        for c in range(2, e_tiles):
             load_old(c)
 
         make_identity(nc, ident[:])
@@ -121,7 +121,7 @@ def tile_attend_passedthrough_written_lean_kernel(
             quantize(q_codes[g][:], q_scales[g][:], q_bf[g][:].rearrange("p q j -> p (q j)"))
         gather_keys(1)
 
-        prod = sb.tile([P, q_tiles, I], F32, name="prod")
+        prod = [sb.tile([P, I], F32, name="prod%d" % g, tag="prod%d" % g, align_bytes=64) for g in range(q_tiles)]
 
         def score(dst, g, h):
             nc.tensor.matmul_mx(
@@ -137,38 +137,31 @@ def tile_attend_passedthrough_written_lean_kernel(
         first, second = slice(0, HALF), slice(HALF, I)
         acc = bank("early0")
         score(acc[:, first], 0, 0)
-        nc.scalar.copy(prod[:, 0, first], acc[:, first])
-        nc.scalar.activation(places[0][:].indirect(half_list(idx2, 0)), prod[:, 0, first], COPY)
+        nc.scalar.copy(prod[0][:, first], acc[:, first])
+        nc.scalar.activation(places[0][:].indirect(half_list(idx2, 0)), prod[0][:, first], COPY)
         acc = bank("early1")
         score(acc[:, first], 1, 0)
-        nc.vector.tensor_copy(prod[:, 1, first], acc[:, first])
-        nc.vector.tensor_copy(places[1][:].indirect(half_list(idx2, 0)), prod[:, 1, first])
+        nc.vector.tensor_copy(prod[1][:, first], acc[:, first])
+        nc.vector.tensor_copy(places[1][:].indirect(half_list(idx2, 0)), prod[1][:, first])
         acc = bank("early0")
         for g in range(q_tiles):
             score(acc[:, g * HALF : (g + 1) * HALF], g, 1)
-        nc.scalar.copy(prod[:, :, second], acc[:].rearrange("q (g i) -> q g i", g=q_tiles))
         for g in range(q_tiles):
-            nc.scalar.activation(places[g][:].indirect(half_list(idx2, 1)), prod[:, g, second], COPY)
+            nc.scalar.copy(prod[g][:, second], acc[:, g * HALF : (g + 1) * HALF])
+        for g in range(q_tiles):
+            nc.scalar.activation(places[g][:].indirect(half_list(idx2, 1)), prod[g][:, second], COPY)
 
-        turned_fade = bank("fade1")
-        nc.tensor.transpose(turned_fade[:, 0:P], fade_blocks[:], ident[:])
-        fade_cols = sb.tile([P, M // P], F32, name="fade_cols")
-        nc.vector.tensor_copy(fade_cols[:], turned_fade[:, 0 : M // P])
-        fade_rows = []
-        for h in range(M // BANK):
-            rows = bank("fade%d" % h)
-            for j in range(PACK):
-                nc.tensor.transpose(
-                    rows[:, j * P : (j + 1) * P], fade_cols[:, PACK * h + j : PACK * h + j + 1].to_broadcast([P, P]), ident[:]
-                )
-            fade_rows.append(rows)
+        for tag in ("q_bf1", "q_codes1"):
+            late = sb.tile([P, M], F32, name="late_" + tag, tag=tag, align_bytes=64)
+            nc.gpsimd.memset(late[:], 0.0)
+            written.append(late)
 
         turned_values = {}
         v_codes = {}
         v_scales = {}
 
         def gather_values(c):
-            picked = sb.tile([P, I], BF16, name="picked%d" % c, align_bytes=64)
+            picked = sb.tile([P, I], BF16, name="picked%d" % c, tag="picked%d" % c, align_bytes=64)
             if c == 0:
                 nc.vector.tensor_copy(picked[:], val_pool[c][:].indirect(idx[:]))
             else:
@@ -183,41 +176,52 @@ def tile_attend_passedthrough_written_lean_kernel(
         v_pairs = {}
 
         def lay_values(pair):
-            v_pairs[pair] = sb.tile([P, 2, P, 2], F32, name="v_bf%d" % pair, align_bytes=64)
+            v_pairs[pair] = sb.tile([P, 2, P, 2], F32, name="v_bf%d" % pair, tag="v_bf1" if pair else "s1", align_bytes=64)
             copy = nc.vector.tensor_copy if pair else nc.scalar.copy
             copy(v_pairs[pair][:], turned_values[pair][:].rearrange("p (k u e) -> p k e u", k=2, u=2))
 
         def quantize_values(pair):
             v_bf = v_pairs[pair]
-            v_codes[pair] = sb.tile([P, 2 * P], U32, name="v_codes%d" % pair, tag="places%d" % (1 - pair), align_bytes=64)
+            v_codes[pair] = sb.tile([P, 2 * P], U32, name="v_codes%d" % pair, align_bytes=64)
             v_scales[pair] = sb.tile([P, 2 * P], U8, name="v_scales%d" % pair, align_bytes=64)
             quantize(v_codes[pair][:], v_scales[pair][:], v_bf[:].rearrange("p k e u -> p (k e u)").bitcast(BF16))
 
         w_codes = sb.tile([P, Q], U32, name="w_codes", align_bytes=64)
         w_scales = sb.tile([P, Q], U8, name="w_scales", align_bytes=64)
 
+        w_bf = sb.tile([P, Q, PACK], BF16, name="w_bf", tag="prod1", align_bytes=64)
+
         def weigh(g):
             s = sb.tile([P, I], F32, name="s%d" % g, tag="s%d" % g, align_bytes=64)
-            nc.vector.tensor_tensor(s[:], places[g][:].indirect(idx3[:]), prod[:, g, :], ADD)
-            w = sb.tile([P, PACK, P], F32, name="w%d" % g, tag="val_pool1" if g else "w0", align_bytes=64)
+            nc.vector.tensor_tensor(s[:], places[g][:].indirect(idx3[:]), prod[g][:], ADD)
+            w = sb.tile([P, PACK, P], F32, name="w%d" % g, align_bytes=64)
             nc.scalar.activation(w[:].rearrange("q t p -> q p t"), s[:].rearrange("q (p t) -> q p t", t=PACK), SIGMOID)
-            turned = bank("early%d" % g)
+            turned = bank("weights%d" % g)
             for t in range(PACK):
                 nc.tensor.transpose(turned[:, t * P : (t + 1) * P], w[:, t, :], ident[:])
-            w_bf = sb.tile([P, P, PACK], BF16, name="w_bf%d" % g, align_bytes=64)
             nc.vector.tensor_tensor(
-                w_bf[:],
+                w_bf[:, g * P : (g + 1) * P, :],
                 turned[:].rearrange("p (t q) -> p q t", t=PACK),
                 factor[:].unsqueeze(1).to_broadcast([P, P, PACK]),
                 MULT,
             )
-            cols = slice(g * P, (g + 1) * P)
-            quantize(w_codes[:, cols], w_scales[:, cols], w_bf[:].rearrange("p q t -> p (q t)"))
+
+        fade_rows = {}
+        for h in reversed(range(M // BANK)):
+            rows = bank("early%d" % (1 - h))
+            for j in range(PACK):
+                nc.tensor.transpose(
+                    rows[:, j * P : (j + 1) * P], fade_cols[:, h, j : j + 1].to_broadcast([P, P]), ident[:]
+                )
+            fade_rows[h] = rows[:].rearrange("e (j n) -> e n j", j=PACK)
 
         gather_values(0)
         weigh(0)
+        fade_right = sb.tile([P, BANK], F32, name="fade_right", tag="places0", align_bytes=64)
+        nc.scalar.copy(fade_right[:].rearrange("e (n j) -> e n j", j=PACK), fade_rows[1])
         gather_values(1)
         weigh(1)
+        quantize(w_codes[:], w_scales[:], w_bf[:].rearrange("p q t -> p (q t)"))
         lay_values(0)
         quantize_values(0)
         gather_values(2)
@@ -225,48 +229,67 @@ def tile_attend_passedthrough_written_lean_kernel(
         lay_values(1)
         quantize_values(1)
 
-        def fade_old(c):
-            for h in range(M // BANK):
-                part = kept[c][:, h * BANK : (h + 1) * BANK]
-                nc.vector.tensor_tensor(part, part, fade_rows[h][:], MULT)
+        faded = [[kept[c][:, h * BANK : (h + 1) * BANK] for h in range(M // BANK)] for c in range(e_tiles)]
 
-        results = []
+        def product(dst, c):
+            cols = slice((c % 2) * P, (c % 2 + 1) * P)
+            nc.tensor.matmul_mx(
+                out=dst,
+                lhsT=v_codes[c // 2][:, cols].bitcast(FP8X4),
+                lhsT_scale=v_scales[c // 2][:, cols],
+                rhs=w_codes[:].bitcast(FP8X4),
+                rhs_scale=w_scales[:],
+                start=True,
+                stop=True,
+            )
 
-        def products(pair):
-            acc = bank("turn%d" % pair)
-            for k in range(2):
-                nc.tensor.matmul_mx(
-                    out=acc[:, k * Q : (k + 1) * Q],
-                    lhsT=v_codes[pair][:, k * P : (k + 1) * P].bitcast(FP8X4),
-                    lhsT_scale=v_scales[pair][:, k * P : (k + 1) * P],
-                    rhs=w_codes[:].bitcast(FP8X4),
-                    rhs_scale=w_scales[:],
-                    start=True,
-                    stop=True,
-                )
-            o = sb.tile([P, 2 * Q], F32, name="o%d" % pair, tag="val_pool%d" % (3 - pair), align_bytes=64)
-            nc.scalar.copy(o[:], acc[:])
-            results.extend(o[:, k * Q : (k + 1) * Q] for k in range(2))
+        acc = bank("weights0")
+        product(acc[:, 0:Q], 0)
+        o0 = sb.tile([P, Q], F32, name="o0", tag="val_pool3", align_bytes=64)
+        nc.scalar.copy(o0[:], acc[:, 0:Q])
+        nc.scalar.activation(written[0][:].indirect(idx4[:]), o0[:], COPY)
+        acc = bank("weights1")
+        product(acc[:, 0:Q], 1)
+        o1 = sb.tile([P, Q], F32, name="o1", tag="picked3", align_bytes=64)
+        nc.vector.tensor_copy(o1[:], acc[:, 0:Q])
+        nc.vector.tensor_copy(written[1][:].indirect(idx4[:]), o1[:])
+        acc = bank("turn0")
+        for k in range(2):
+            product(acc[:, k * Q : (k + 1) * Q], 2 + k)
+        o23 = sb.tile([P, 2, Q], F32, name="o23")
+        nc.scalar.copy(o23[:], acc[:].rearrange("e (k q) -> e k q", k=2))
+        for k in range(2):
+            nc.scalar.activation(written[2 + k][:].indirect(idx4[:]), o23[:, k, :], COPY)
 
-        def write(c):
-            nc.scalar.activation(written[c % WINDOWS][:].indirect(idx4[:]), results[c], COPY)
+        early_left = sb.tile([P, 2, BANK], F32, name="early_left", tag="places1", align_bytes=64)
+        for c in range(e_tiles):
+            left = faded[c][0]
+            if c < 2:
+                faded[c][0] = early_left[:, c, :]
+            nc.vector.tensor_tensor(
+                faded[c][0].rearrange("e (n j) -> e n j", j=PACK),
+                left.rearrange("e (n j) -> e n j", j=PACK),
+                fade_rows[0],
+                MULT,
+            )
+            right = faded[c][1]
+            if c == 2:
+                faded[c][1] = sb.tile([P, BANK], F32, name="faded2", tag="prod1", align_bytes=64)[:]
+            nc.gpsimd.tensor_tensor(faded[c][1], right, fade_right[:], MULT)
 
-        def finish(c, width):
+        def finish(c, width, dst):
             for col in range(0, M, width):
                 cols = slice(col, col + width)
-                nc.vector.tensor_tensor(kept[c][:, cols], kept[c][:, cols], written[c % WINDOWS][:, cols], ADD)
-                nc.sync.dma_start(out[c * P : (c + 1) * P, cols], kept[c][:, cols])
+                part = faded[c][col // BANK][:, col % BANK : col % BANK + width]
+                nc.vector.tensor_tensor(dst[:, cols], part, written[c][:, cols], ADD)
+                nc.sync.dma_start(out[c * P : (c + 1) * P, cols], dst[:, cols])
 
-        products(0)
-        write(0)
-        write(1)
-        products(1)
-        for c in range(3):
-            fade_old(c)
-        finish(0, M)
-        write(2)
-        finish(1, M)
-        write(3)
-        fade_old(3)
-        finish(2, BANK)
-        finish(3, BANK // 2)
+        right = slice(BANK, M)
+        nc.gpsimd.tensor_tensor(kept[0][:, right], faded[0][1], written[0][:, right], ADD)
+        nc.sync.dma_start(out[0:P, right], kept[0][:, right])
+        first_out = sb.tile([P, BANK], F32, name="first_out", tag="picked3", align_bytes=64)
+        nc.vector.tensor_tensor(first_out[:], faded[0][0], written[0][:, 0:BANK], ADD)
+        nc.sync.dma_start(out[0:P, 0:BANK], first_out[:])
+        finish(1, BANK, kept[1])
+        finish(2, BANK, kept[2])
+        finish(3, BANK // 2, kept[3])

from contextlib import ExitStack

import concourse.mybir as mybir
from concourse.masks import make_identity

D, T, I, Q, E, Z, M = 512, 2048, 512, 256, 512, 1024, 1024
FLOPS = 2 * D * Q * I + 2 * I * E * Q

F32 = mybir.dt.float32
BF16 = mybir.dt.bfloat16
I32 = mybir.dt.int32
U32 = mybir.dt.uint32
U16 = mybir.dt.uint16
U8 = mybir.dt.uint8
FP8X4 = mybir.dt.float8_e4m3fn_x4
FP4X4 = mybir.dt.float4_e2m1fn_x4
MULT = mybir.AluOpType.mult
ADD = mybir.AluOpType.add
COPY = mybir.ActivationFunctionType.Copy
SIGMOID = mybir.ActivationFunctionType.Sigmoid

P = 128
PACK = 4
BANK = 512
HALF = I // 2
LIST_ROWS = 16
WINDOWS = 2


def tile_attend_passedthrough_written_lean_kernel(
    tc, query, keys_words, keys_scales, slot_factor, vals, old, fade, offs, offs2, offs3, offs4, out
):
    nc = tc.nc
    q_tiles = Q // P
    e_tiles = E // P
    with ExitStack() as ctx:
        sb = ctx.enter_context(tc.tile_pool(name="sb", bufs=1))
        ps = ctx.enter_context(tc.psum_pool(name="ps", bufs=1))

        def bank(tag):
            return ps.tile([P, BANK], F32, name=tag, tag=tag)

        idx = sb.tile([P, I // LIST_ROWS], U16, name="idx")
        idx2 = sb.tile([P, I // LIST_ROWS], U16, name="idx2")
        idx3 = sb.tile([P, I // LIST_ROWS], U16, name="idx3")
        idx4 = sb.tile([P, Q // LIST_ROWS], U16, name="idx4")
        key_words = sb.tile([P, T], U16, name="key_words", align_bytes=64)
        key_scales = sb.tile([P, T], U8, name="key_scales", align_bytes=64)
        query_raw = [sb.tile([P, PACK, P], F32, name="query_raw%d" % g, tag="query_raw%d" % g, align_bytes=64) for g in range(q_tiles)]
        factor = sb.tile([P, PACK], F32, name="factor")
        fade_cols = sb.tile([P, M // BANK, PACK], F32, name="fade_cols")
        val_pool = [sb.tile([P, T], F32, name="val_pool%d" % c, tag="val_pool%d" % c, align_bytes=64) for c in range(e_tiles)]
        kept = [sb.tile([P, M], F32, name="kept%d" % c) for c in range(e_tiles)]
        places = [sb.tile([P, Z], F32, name="places%d" % g, tag="places%d" % g, align_bytes=64) for g in range(q_tiles)]
        written = [sb.tile([P, M], F32, name="written%d" % c, tag="written%d" % c) for c in range(WINDOWS)]
        ident = sb.tile([P, P], F32, name="ident")

        nc.gpsimd.memset(key_scales[:].bitcast(I32), 0)
        nc.sync.dma_start(idx[:], offs)
        nc.sync.dma_start(idx2[:], offs2)
        nc.sync.dma_start(key_words[:].bitcast(I32), keys_words[0].bitcast(I32))
        for quad in range(4):
            nc.sync.dma_start(
                key_scales[32 * quad : 32 * quad + 4, :].bitcast(I32),
                keys_scales[0, 4 * quad : 4 * quad + 4, :].bitcast(I32),
            )
        for g in range(q_tiles):
            nc.sync.dma_start(query_raw[g][:], query[:, g * P : (g + 1) * P].rearrange("(p j) q -> p j q", j=PACK))

        def load_values(c):
            nc.sync.dma_start(val_pool[c][:], vals[c * P : (c + 1) * P, :])

        def load_old(c):
            nc.sync.dma_start(kept[c][:], old[c * P : (c + 1) * P, :])

        load_values(0)
        nc.sync.dma_start(fade_cols[:], fade[0].rearrange("(h p j) -> p h j", p=P, j=PACK))
        load_values(1)
        nc.sync.dma_start(factor[:], slot_factor[0].rearrange("(p t) -> p t", t=PACK))
        load_old(0)
        nc.sync.dma_start(idx3[:], offs3)
        load_old(1)
        load_values(2)
        nc.sync.dma_start(idx4[:], offs4)
        load_values(3)
        for c in range(2, e_tiles):
            load_old(c)

        make_identity(nc, ident[:])
        warm = sb.tile([P, 1], F32, name="warm")
        nc.scalar.activation(warm[:], ident[:, 0:1], SIGMOID)
        for g in range(q_tiles):
            nc.vector.memset(places[g][:], 0.0)
        for c in range(WINDOWS):
            nc.vector.memset(written[c][:], 0.0)

        q_bf = [sb.tile([P, P, PACK], BF16, name="q_bf%d" % g, tag="q_bf%d" % g, align_bytes=64) for g in range(q_tiles)]
        q_codes = [sb.tile([P, P], U32, name="q_codes%d" % g, tag="q_codes%d" % g, align_bytes=64) for g in range(q_tiles)]
        q_scales = [sb.tile([P, P], U8, name="q_scales%d" % g, align_bytes=64) for g in range(q_tiles)]
        got_words = []
        got_scales = []

        def half_list(lst, h):
            return lst[:, h * HALF // LIST_ROWS : (h + 1) * HALF // LIST_ROWS]

        def gather_keys(h):
            words = sb.tile([P, HALF], U16, name="got_words%d" % h, tag="q_bf0" if h else "got_words", align_bytes=64)
            scales = sb.tile([P, HALF], U8, name="got_scales%d" % h, tag="query_raw0" if h else "got_scales", align_bytes=64)
            nc.vector.tensor_copy(words[:], key_words[:].indirect(half_list(idx, h)))
            nc.vector.tensor_copy(scales[:], key_scales[:].indirect(half_list(idx, h)))
            got_words.append(words)
            got_scales.append(scales)

        def quantize(codes, scales, rounded):
            nc.vector.quantize_mx(out=codes.bitcast(FP8X4), scales=scales, in_=rounded)

        for g in range(q_tiles):
            nc.scalar.copy(q_bf[g][:], query_raw[g][:].rearrange("p j q -> p q j"))
        gather_keys(0)
        for g in range(q_tiles):
            quantize(q_codes[g][:], q_scales[g][:], q_bf[g][:].rearrange("p q j -> p (q j)"))
        gather_keys(1)

        prod = [sb.tile([P, I], F32, name="prod%d" % g, tag="prod%d" % g, align_bytes=64) for g in range(q_tiles)]

        def score(dst, g, h):
            nc.tensor.matmul_mx(
                out=dst,
                lhsT=q_codes[g][:].bitcast(FP8X4),
                lhsT_scale=q_scales[g][:],
                rhs=got_words[h][:].bitcast(FP4X4),
                rhs_scale=got_scales[h][:],
                start=True,
                stop=True,
            )

        first, second = slice(0, HALF), slice(HALF, I)
        acc = bank("early0")
        score(acc[:, first], 0, 0)
        nc.scalar.copy(prod[0][:, first], acc[:, first])
        nc.scalar.activation(places[0][:].indirect(half_list(idx2, 0)), prod[0][:, first], COPY)
        acc = bank("early1")
        score(acc[:, first], 1, 0)
        nc.vector.tensor_copy(prod[1][:, first], acc[:, first])
        nc.vector.tensor_copy(places[1][:].indirect(half_list(idx2, 0)), prod[1][:, first])
        acc = bank("early0")
        for g in range(q_tiles):
            score(acc[:, g * HALF : (g + 1) * HALF], g, 1)
        for g in range(q_tiles):
            nc.scalar.copy(prod[g][:, second], acc[:, g * HALF : (g + 1) * HALF])
        for g in range(q_tiles):
            nc.scalar.activation(places[g][:].indirect(half_list(idx2, 1)), prod[g][:, second], COPY)

        for tag in ("q_bf1", "q_codes1"):
            late = sb.tile([P, M], F32, name="late_" + tag, tag=tag, align_bytes=64)
            nc.gpsimd.memset(late[:], 0.0)
            written.append(late)

        turned_values = {}
        v_codes = {}
        v_scales = {}

        def gather_values(c):
            picked = sb.tile([P, I], BF16, name="picked%d" % c, tag="picked%d" % c, align_bytes=64)
            if c == 0:
                nc.vector.tensor_copy(picked[:], val_pool[c][:].indirect(idx[:]))
            else:
                nc.scalar.activation(picked[:], val_pool[c][:].indirect(idx[:]), COPY)
            pairs = picked[:].bitcast(F32)
            if c % 2 == 0:
                turned_values[c // 2] = bank("turn%d" % (c // 2))
            for u in range(2):
                col = (2 * (c % 2) + u) * P
                nc.tensor.transpose(turned_values[c // 2][:, col : col + P], pairs[:, u : I // 2 : 2], ident[:])

        v_pairs = {}

        def lay_values(pair):
            v_pairs[pair] = sb.tile([P, 2, P, 2], F32, name="v_bf%d" % pair, tag="v_bf1" if pair else "s1", align_bytes=64)
            copy = nc.vector.tensor_copy if pair else nc.scalar.copy
            copy(v_pairs[pair][:], turned_values[pair][:].rearrange("p (k u e) -> p k e u", k=2, u=2))

        def quantize_values(pair):
            v_bf = v_pairs[pair]
            v_codes[pair] = sb.tile([P, 2 * P], U32, name="v_codes%d" % pair, align_bytes=64)
            v_scales[pair] = sb.tile([P, 2 * P], U8, name="v_scales%d" % pair, align_bytes=64)
            quantize(v_codes[pair][:], v_scales[pair][:], v_bf[:].rearrange("p k e u -> p (k e u)").bitcast(BF16))

        w_codes = sb.tile([P, Q], U32, name="w_codes", align_bytes=64)
        w_scales = sb.tile([P, Q], U8, name="w_scales", align_bytes=64)

        w_bf = sb.tile([P, Q, PACK], BF16, name="w_bf", tag="prod1", align_bytes=64)

        def weigh(g):
            s = sb.tile([P, I], F32, name="s%d" % g, tag="s%d" % g, align_bytes=64)
            nc.vector.tensor_tensor(s[:], places[g][:].indirect(idx3[:]), prod[g][:], ADD)
            w = sb.tile([P, PACK, P], F32, name="w%d" % g, align_bytes=64)
            nc.scalar.activation(w[:].rearrange("q t p -> q p t"), s[:].rearrange("q (p t) -> q p t", t=PACK), SIGMOID)
            turned = bank("weights%d" % g)
            for t in range(PACK):
                nc.tensor.transpose(turned[:, t * P : (t + 1) * P], w[:, t, :], ident[:])
            nc.vector.tensor_tensor(
                w_bf[:, g * P : (g + 1) * P, :],
                turned[:].rearrange("p (t q) -> p q t", t=PACK),
                factor[:].unsqueeze(1).to_broadcast([P, P, PACK]),
                MULT,
            )

        fade_rows = {}
        for h in reversed(range(M // BANK)):
            rows = bank("early%d" % (1 - h))
            for j in range(PACK):
                nc.tensor.transpose(
                    rows[:, j * P : (j + 1) * P], fade_cols[:, h, j : j + 1].to_broadcast([P, P]), ident[:]
                )
            fade_rows[h] = rows[:].rearrange("e (j n) -> e n j", j=PACK)

        gather_values(0)
        weigh(0)
        fade_right = sb.tile([P, BANK], F32, name="fade_right", tag="places0", align_bytes=64)
        nc.scalar.copy(fade_right[:].rearrange("e (n j) -> e n j", j=PACK), fade_rows[1])
        gather_values(1)
        weigh(1)
        quantize(w_codes[:], w_scales[:], w_bf[:].rearrange("p q t -> p (q t)"))
        lay_values(0)
        quantize_values(0)
        gather_values(2)
        gather_values(3)
        lay_values(1)
        quantize_values(1)

        faded = [[kept[c][:, h * BANK : (h + 1) * BANK] for h in range(M // BANK)] for c in range(e_tiles)]

        def product(dst, c):
            cols = slice((c % 2) * P, (c % 2 + 1) * P)
            nc.tensor.matmul_mx(
                out=dst,
                lhsT=v_codes[c // 2][:, cols].bitcast(FP8X4),
                lhsT_scale=v_scales[c // 2][:, cols],
                rhs=w_codes[:].bitcast(FP8X4),
                rhs_scale=w_scales[:],
                start=True,
                stop=True,
            )

        acc = bank("weights0")
        product(acc[:, 0:Q], 0)
        o0 = sb.tile([P, Q], F32, name="o0", tag="val_pool3", align_bytes=64)
        nc.scalar.copy(o0[:], acc[:, 0:Q])
        nc.scalar.activation(written[0][:].indirect(idx4[:]), o0[:], COPY)
        acc = bank("weights1")
        product(acc[:, 0:Q], 1)
        o1 = sb.tile([P, Q], F32, name="o1", tag="picked3", align_bytes=64)
        nc.vector.tensor_copy(o1[:], acc[:, 0:Q])
        nc.vector.tensor_copy(written[1][:].indirect(idx4[:]), o1[:])
        acc = bank("turn0")
        for k in range(2):
            product(acc[:, k * Q : (k + 1) * Q], 2 + k)
        o23 = sb.tile([P, 2, Q], F32, name="o23")
        nc.scalar.copy(o23[:], acc[:].rearrange("e (k q) -> e k q", k=2))
        for k in range(2):
            nc.scalar.activation(written[2 + k][:].indirect(idx4[:]), o23[:, k, :], COPY)

        early_left = sb.tile([P, 2, BANK], F32, name="early_left", tag="places1", align_bytes=64)
        for c in range(e_tiles):
            left = faded[c][0]
            if c < 2:
                faded[c][0] = early_left[:, c, :]
            nc.vector.tensor_tensor(
                faded[c][0].rearrange("e (n j) -> e n j", j=PACK),
                left.rearrange("e (n j) -> e n j", j=PACK),
                fade_rows[0],
                MULT,
            )
            right = faded[c][1]
            if c == 2:
                faded[c][1] = sb.tile([P, BANK], F32, name="faded2", tag="prod1", align_bytes=64)[:]
            nc.gpsimd.tensor_tensor(faded[c][1], right, fade_right[:], MULT)

        def finish(c, width, dst):
            for col in range(0, M, width):
                cols = slice(col, col + width)
                part = faded[c][col // BANK][:, col % BANK : col % BANK + width]
                nc.vector.tensor_tensor(dst[:, cols], part, written[c][:, cols], ADD)
                nc.sync.dma_start(out[c * P : (c + 1) * P, cols], dst[:, cols])

        right = slice(BANK, M)
        nc.gpsimd.tensor_tensor(kept[0][:, right], faded[0][1], written[0][:, right], ADD)
        nc.sync.dma_start(out[0:P, right], kept[0][:, right])
        first_out = sb.tile([P, BANK], F32, name="first_out", tag="picked3", align_bytes=64)
        nc.vector.tensor_tensor(first_out[:], faded[0][0], written[0][:, 0:BANK], ADD)
        nc.sync.dma_start(out[0:P, 0:BANK], first_out[:])
        finish(1, BANK, kept[1])
        finish(2, BANK, kept[2])
        finish(3, BANK // 2, kept[3])
